import numpy as np
import ml_dtypes


def mxq(x, axis, fmt="e4m3"):
    dtype, down = {"e4m3": (ml_dtypes.float8_e4m3fn, 7), "e5m2": (ml_dtypes.float8_e5m2, 14)}[fmt]
    v = np.moveaxis(np.asarray(x, np.float32).astype(ml_dtypes.bfloat16).astype(np.float64), axis, -1)
    blocks = v.reshape(v.shape[:-1] + (-1, 32))
    amax = np.abs(blocks).max(-1, keepdims=True)
    byte = np.maximum(np.where(amax > 0, np.frexp(amax)[1] - 1 + 127, 0) - down, 1)
    scale = np.exp2(byte - 127.0)
    codes = (blocks / scale).astype(np.float32).astype(dtype).astype(np.float64)
    return np.moveaxis((codes * scale).reshape(v.shape), -1, axis)


WIDE = False


def mx_kscale(k):
    if not WIDE:
        return np.ones(k)
    levels = np.array([10, -10, 5, -5, 0])
    if k % 512:
        return np.exp2(np.random.permutation(np.resize(levels, k // 32))).repeat(32)
    a = np.empty((k // 512, 16))
    for p in range(k // 512):
        a[p, :8] = np.random.permutation(np.resize(levels, 8))
        for g in range(8):
            far = levels[np.abs(levels - a[p, g]) >= 10]
            a[p, g + 8] = far[np.random.randint(len(far))]
    return np.exp2(a.ravel()).repeat(32)


def f64(x):
    return np.asarray(x).astype(np.float64)


def striped(idx):
    return np.tile(idx.reshape(-1, 16).T, (8, 1)).astype(np.uint16)


def unstriped(offs):
    return offs[:16].T.reshape(-1).astype(np.int64)


def pack_weight(w):
    k, n = w.shape
    w = f64(np.asarray(w, np.float32).astype(ml_dtypes.bfloat16)).reshape(k // 32, 32, n)
    amax = np.abs(w).max(1)
    byte = np.clip(np.where(amax > 0, np.frexp(amax)[1] - 1 + 127 - 7, 1), 1, 254)
    scaled = (w * np.exp2(127.0 - byte)[:, None, :]).reshape(k, n).astype(np.float32)
    words = np.ascontiguousarray(scaled.reshape(k // 512, 128, 4, n).transpose(0, 1, 3, 2)).astype(ml_dtypes.float8_e4m3fn).view(np.uint8)
    return words, np.ascontiguousarray(byte.astype(np.uint8).reshape(k // 512, 16, n))


def unpack_weight(words, scales):
    g, p, n, _ = words.shape
    vals = np.ascontiguousarray(words).view(ml_dtypes.float8_e4m3fn).astype(np.float64) * np.repeat(np.exp2(scales.astype(np.float64) - 127.0), 8, axis=1)[..., None]
    return vals.transpose(0, 1, 3, 2).reshape(g * 512, n)


def sigmoid(v):
    return 1.0 / (1.0 + np.exp(-np.maximum(v, -700.0)))


K, T, S, N, H = 1024, 2048, 512, 256, 512


def setup_inputs():
    n = np.random.standard_normal
    s = mx_kscale(K)[:, None]
    u = mx_kscale(H)
    packed_xT = pack_weight(n((K, T)) * s)
    return {
        "x_words": packed_xT[0],
        "x_scales": packed_xT[1],
        "w1": (n((K, H)) / np.sqrt(K) / s).astype(np.float32),
        "w2": (n((K, H)) / np.sqrt(K) / s).astype(np.float32),
        "dust": (np.random.uniform(0.1, 0.5, (H, S))).astype(np.float32),
        "unit": (np.random.uniform(0.6, 1.4, (H, 1)) * u[:, None]).astype(np.float32),
        "w3": (n((H, N)) / np.sqrt(H) / u[:, None]).astype(np.float32),
        "offs": striped(np.random.permutation(T)[:S]),
        "src": striped(np.random.permutation(S)),
    }


def reference(x_words, x_scales, w1, w2, dust, unit, w3, offs, src):
    xq = unpack_weight(x_words, x_scales)[:, unstriped(offs)]
    ts = mxq(f64(w1), 0, "e4m3").T @ xq
    melt = sigmoid(2.0 * ts)
    ag = mxq(f64(w2), 0, "e4m3").T @ xq
    age = np.log(np.exp(ag) + 1.0)
    cold = (-1.0 * melt + 1.0) * np.exp(-1.0 * age)
    wet = melt * np.exp(-1.8 * age)
    as_ = age[:, unstriped(src)]
    dst = as_ * f64(dust)
    alb = (cold + wet + 0.2) / (dst + 1.0)
    hid = f64(unit) * alb
    return mxq(f64(w3), 0, "e4m3").T @ mxq(hid, 0, "e4m3")

@@ -1,0 +1,219 @@
+from contextlib import ExitStack
+
+import concourse.mybir as mybir
+
+K, T, S, N, H = 1024, 2048, 512, 256, 512
+FLOPS = 2 * (2 * K * H * S + H * N * S)
+
+F32 = mybir.dt.float32
+BF16 = mybir.dt.bfloat16
+I32 = mybir.dt.int32
+U32 = mybir.dt.uint32
+U16 = mybir.dt.uint16
+U8 = mybir.dt.uint8
+FP8X4 = mybir.dt.float8_e4m3fn_x4
+ACT = mybir.ActivationFunctionType
+ALU = mybir.AluOpType
+
+P = 128
+PACK = 4
+PASSES = K // (P * PACK)
+HALF = S // 2
+CHUNKS = ((0, 256), (256, 128), (384, 128))
+TINY = 2.0 ** -60
+
+
+def tile_picked_ysnowa_alb_p_kernel(tc, x_words, x_scales, w1, w2, dust, unit, w3, offs, src, out):
+    nc = tc.nc
+    with ExitStack() as ctx:
+        keep = ctx.enter_context(tc.tile_pool(name="keep", bufs=1))
+        psum = ctx.enter_context(tc.psum_pool(name="psum", bufs=1))
+
+        def sb(shape, dtype, name):
+            return keep.tile(shape, dtype, name=name, align_bytes=64)
+
+        offs_t = keep.tile([P, S // 16], U16, name="offs_t")
+        src_t = keep.tile([P, S // 16], U16, name="src_t")
+        nc.sync.dma_start(offs_t[:], offs)
+
+        xs = sb([P, PASSES * T], U8, "xs")
+        nc.gpsimd.memset(xs[:, :T].bitcast(I32), 0)
+        nc.vector.memset(xs[:, T:].bitcast(I32), 0)
+        consts = sb([P, 2], F32, "consts")
+        nc.vector.memset(consts[:, 0:1], 1.0)
+        nc.vector.memset(consts[:, 1:2], TINY)
+        one, tiny = consts[:, 0:1], consts[:, 1:2]
+        scale_rows = x_scales.bitcast(I32).rearrange("g (q r) c -> r q g c", r=4)
+
+        def load_w(w, g, c0, c1, name):
+            raw = sb([P, PACK, c1 - c0], F32, name)
+            nc.sync.dma_start(raw[:], w[512 * g:512 * (g + 1), c0:c1].rearrange("(p j) c -> p j c", j=PACK))
+            return raw
+
+        def load_x(g):
+            words = sb([P, T], I32, f"xw{g}")
+            nc.sync.dma_start(words[:], x_words[g].rearrange("p n t -> p (n t)").bitcast(I32))
+            return words
+
+        w2_raw = [load_w(w2, 0, 0, H, "w2_raw0")]
+        for r in range(4):
+            nc.sync.dma_start(xs[r:P:32, :].bitcast(I32).rearrange("q (g c) -> q g c", g=PASSES), scale_rows[r])
+        xw = [load_x(0)]
+        w2_raw.append(load_w(w2, 1, 0, H, "w2_raw1"))
+        xw.append(load_x(1))
+        w1_raw = [[load_w(w1, g, 256 * h, 256 * (h + 1), f"w1_raw{g}{h}") for h in range(2)] for g in range(PASSES)]
+        w3_raw = sb([P, PACK, N], F32, "w3_raw")
+        nc.sync.dma_start(w3_raw[:], w3.rearrange("(p j) c -> p j c", j=PACK))
+        nc.sync.dma_start(src_t[:], src)
+        dust_rows = dust.rearrange("(p t) j -> t p j", t=PACK)
+        dust_t = []
+        for t in range(PACK):
+            d_ = sb([P, S], F32, f"dust{t}")
+            nc.sync.dma_start(d_[:], dust_rows[t])
+            dust_t.append(d_)
+        unit_t = sb([P, PACK], F32, "unit_t")
+        nc.sync.dma_start(unit_t[:], unit.rearrange("(p t) o -> p (t o)", t=PACK))
+
+        def deal(copy, grouped, raw, m0):
+            width = raw.shape[2] // PACK
+            copy(grouped[:].rearrange("p (t m j) -> p m j t", t=PACK, j=PACK)[:, m0:m0 + width],
+                 raw[:].rearrange("p j (m t) -> p m j t", t=PACK))
+
+        def quantise(grouped, name):
+            width = grouped.shape[1] // PACK
+            codes = sb([P, width], U32, name + "_codes")
+            scales = sb([P, width], U8, name + "_scales")
+            nc.vector.quantize_mx(out=codes[:].bitcast(FP8X4), scales=scales[:], in_=grouped[:])
+            return codes, scales
+
+        def interleave(copy, grouped, planes):
+            copy(grouped[:].rearrange("p (c i t) -> p c t i", t=PACK, i=4),
+                 planes[:].rearrange("p t (c i) -> p c t i", i=4))
+
+        w2_g = [sb([P, PACK * H], BF16, f"w2_g{g}") for g in range(PASSES)]
+        for g in range(PASSES):
+            deal(nc.scalar.copy, w2_g[g], w2_raw[g], 0)
+        gs, gw, w2_q = [], [], []
+        for g in range(PASSES):
+            s_ = sb([P, S], U8, f"gs{g}")
+            nc.vector.tensor_copy(s_[:], xs[:, g * T:(g + 1) * T].indirect(offs_t[:]))
+            gs.append(s_)
+        for g in range(PASSES):
+            w2_q.append(quantise(w2_g[g], f"w2_{g}"))
+            c_ = sb([P, S], U32, f"gw{g}")
+            nc.vector.tensor_copy(c_[:], xw[g][:].bitcast(U32).indirect(offs_t[:]))
+            gw.append(c_)
+
+        def product(wq, tag):
+            banks = [psum.tile([P, S], F32, name=f"{tag}{t}", tag=f"{tag}{t}") for t in range(PACK)]
+            for g in range(PASSES):
+                for t in range(PACK):
+                    cols = slice(P * t, P * (t + 1))
+                    nc.tensor.matmul_mx(out=banks[t][:], lhsT=wq[g][0][:, cols].bitcast(FP8X4), lhsT_scale=wq[g][1][:, cols],
+                                        rhs=gw[g][:].bitcast(FP8X4), rhs_scale=gs[g][:],
+                                        start=(g == 0), stop=(g == PASSES - 1))
+            return banks
+
+        ag = product(w2_q, "ag")
+        u = sb([P, PACK, S], F32, "u")
+        for t in range(PACK):
+            nc.scalar.activation(u[:, t, :], ag[t][:], ACT.Sigmoid, scale=-1.0)
+
+        w1_g = [sb([P, PACK * H], BF16, f"w1_g{g}") for g in range(PASSES)]
+        w1_q = []
+        for g in range(PASSES):
+            for h in range(2):
+                deal(nc.vector.tensor_copy, w1_g[g], w1_raw[g][h], 64 * h)
+            w1_q.append(quantise(w1_g[g], f"w1_{g}"))
+        ts = product(w1_q, "ts")
+        w3_g = sb([P, PACK * N], BF16, "w3_g")
+        interleave(nc.vector.tensor_copy, w3_g, w3_raw)
+        w3_q = quantise(w3_g, "w3")
+
+        lnu = sb([P, PACK, S], F32, "lnu")
+        for t in range(PACK):
+            nc.scalar.activation(lnu[:, t, :], u[:, t, :], ACT.Ln, bias=tiny)
+        wr = sb([P, PACK, S], F32, "wr")
+        for t in range(0, PACK, 2):
+            nc.scalar.activation(wr[:, t:t + 2, :], lnu[:, t:t + 2, :], ACT.Exp, scale=0.8)
+        melt = sb([P, PACK, S], F32, "melt")
+        for t in range(PACK):
+            nc.scalar.activation(melt[:, t, :], ts[t][:], ACT.Sigmoid, scale=2.0)
+
+        age = [sb([P, S + 16], F32, f"age{t}") for t in range(PACK)]
+        for t in range(PACK):
+            nc.gpsimd.memset(age[t][:, S:], 0.0)
+        dst = sb([P, PACK, S], F32, "dst")
+
+        def make_age(t):
+            nc.vector.scalar_tensor_tensor(age[t][:, :S], lnu[:, t, :], -1.0, ag[t][:], ALU.mult, ALU.max)
+
+        make_age(0)
+        for t in range(PACK):
+            if t + 1 < PACK:
+                make_age(t + 1)
+            nc.vector.tensor_tensor(dst[:, t, :], age[t][:].indirect(src_t[:]), dust_t[t][:], ALU.mult)
+
+        den2 = sb([P, PACK, S], F32, "den2")
+        for t in range(PACK):
+            nc.scalar.activation(den2[:, t, :], dst[:, t, :], ACT.Square, bias=one)
+        rec = sb([P, PACK, S], F32, "rec")
+        for c0, cw in CHUNKS:
+            nc.scalar.activation(rec[:, :, c0:c0 + cw], den2[:, :, c0:c0 + cw], ACT.Abs_reciprocal_sqrt)
+
+        unit2 = sb([P, PACK], F32, "unit2")
+        nc.vector.tensor_scalar(unit2[:], unit_t[:], 2.0, None, ALU.mult)
+        sgn = sb([P, PACK, S], F32, "sgn")
+        for t in range(0, PACK, 2):
+            nc.vector.tensor_scalar(sgn[:, t:t + 2, :], dst[:, t:t + 2, :], -1.0, 0.5, ALU.is_ge, ALU.subtract)
+        pa = sb([P, PACK, S], F32, "pa")
+        pb = sb([P, PACK, S], F32, "pb")
+        for t in range(0, PACK, 2):
+            nc.vector.scalar_tensor_tensor(pa[:, t:t + 2, :], wr[:, t:t + 2, :], -1.0, melt[:, t:t + 2, :], ALU.add, ALU.mult)
+        for t in range(0, PACK, 2):
+            nc.vector.scalar_tensor_tensor(pb[:, t:t + 2, :], pa[:, t:t + 2, :], 1.0, u[:, t:t + 2, :], ALU.add, ALU.mult)
+        num = sb([P, PACK, S], F32, "num")
+
+        def make_num(n):
+            c0, cw = CHUNKS[n]
+            cols = slice(c0, c0 + cw)
+            nc.vector.scalar_tensor_tensor(num[:, :, cols], pb[:, :, cols], 0.2, sgn[:, :, cols], ALU.add, ALU.mult)
+
+        def make_hid(n):
+            c0, cw = CHUNKS[n]
+            z = sb([P, PACK, cw], F32, f"hid{n}")
+            for t in range(PACK):
+                nc.vector.scalar_tensor_tensor(z[:, t, :], num[:, t, c0:c0 + cw], unit2[:, t:t + 1], rec[:, t, c0:c0 + cw],
+                                               ALU.mult, ALU.mult)
+            return z
+
+        def group(n, z):
+            zg = sb([P, PACK * CHUNKS[n][1]], BF16, f"hid_g{n}")
+            interleave(nc.vector.tensor_copy if n == len(CHUNKS) - 1 else nc.scalar.copy, zg, z)
+            return zg
+
+        def finish(n, zg):
+            c0, cw = CHUNKS[n]
+            codes, scales = quantise(zg, f"hid{n}")
+            for b in range(N // P):
+                acc = psum.tile([P, cw], F32, name=f"acc{n}{b}", tag=f"ag{(2 * n + b) % PACK}")
+                cols = slice(P * b, P * (b + 1))
+                nc.tensor.matmul_mx(out=acc[:], lhsT=w3_q[0][:, cols].bitcast(FP8X4), lhsT_scale=w3_q[1][:, cols],
+                                    rhs=codes[:].bitcast(FP8X4), rhs_scale=scales[:], start=True, stop=True)
+                res = sb([P, cw], F32, f"res{n}{b}")
+                if b == 1 and n == len(CHUNKS) - 1:
+                    nc.vector.tensor_copy(res[:], acc[:])
+                else:
+                    nc.scalar.copy(res[:], acc[:])
+                nc.sync.dma_start(out[cols, c0:c0 + cw], res[:])
+
+        make_num(0)
+        make_num(1)
+        g0 = group(0, make_hid(0))
+        make_num(2)
+        g1 = group(1, make_hid(1))
+        z2 = make_hid(2)
+        finish(0, g0)
+        g2 = group(2, z2)
+        finish(1, g1)
+        finish(2, g2)

@@ -55,11 +55,10 @@ def tile_picked_ysnowa_alb_p_kernel(tc, x_words, x_scales, w1, w2, dust, unit, w
             nc.sync.dma_start(words[:], x_words[g].rearrange("p n t -> p (n t)").bitcast(I32))
             return words
 
-        w2_raw = [load_w(w2, 0, 0, H, "w2_raw0")]
+        xw = [load_x(0)]
         for r in range(4):
             nc.sync.dma_start(xs[r:P:32, :].bitcast(I32).rearrange("q (g c) -> q g c", g=PASSES), scale_rows[r])
-        xw = [load_x(0)]
-        w2_raw.append(load_w(w2, 1, 0, H, "w2_raw1"))
+        w2_raw = [load_w(w2, g, 0, H, f"w2_raw{g}") for g in range(PASSES)]
         xw.append(load_x(1))
         w1_raw = [[load_w(w1, g, 256 * h, 256 * (h + 1), f"w1_raw{g}{h}") for h in range(2)] for g in range(PASSES)]
         w3_raw = sb([P, PACK, N], F32, "w3_raw")
@@ -77,7 +76,7 @@ def tile_picked_ysnowa_alb_p_kernel(tc, x_words, x_scales, w1, w2, dust, unit, w
         def deal(copy, grouped, raw, m0):
             width = raw.shape[2] // PACK
             copy(grouped[:].rearrange("p (t m j) -> p m j t", t=PACK, j=PACK)[:, m0:m0 + width],
-                 raw[:].rearrange("p j (m t) -> p m j t", t=PACK))
+                 raw.rearrange("p j (m t) -> p m j t", t=PACK))
 
         def quantise(grouped, name):
             width = grouped.shape[1] // PACK
@@ -92,29 +91,39 @@ def tile_picked_ysnowa_alb_p_kernel(tc, x_words, x_scales, w1, w2, dust, unit, w
 
         w2_g = [sb([P, PACK * H], BF16, f"w2_g{g}") for g in range(PASSES)]
         for g in range(PASSES):
-            deal(nc.scalar.copy, w2_g[g], w2_raw[g], 0)
-        gs, gw, w2_q = [], [], []
+            deal(nc.scalar.copy, w2_g[g], w2_raw[g][:, :, :256], 0)
+        def pick_words(g):
+            picked = sb([P, S], U32, f"gw{g}")
+            pieces = 1 + g
+            for h in range(pieces):
+                a, b = S * h // pieces, S * (h + 1) // pieces
+                nc.vector.tensor_copy(picked[:, a:b], xw[g][:].bitcast(U32).indirect(offs_t[:, a // 16:b // 16]))
+            return picked
+
+        gw = [pick_words(0)]
+        gs = []
         for g in range(PASSES):
             s_ = sb([P, S], U8, f"gs{g}")
             nc.vector.tensor_copy(s_[:], xs[:, g * T:(g + 1) * T].indirect(offs_t[:]))
             gs.append(s_)
+        w2_q = []
         for g in range(PASSES):
+            deal(nc.vector.tensor_copy, w2_g[g], w2_raw[g][:, :, 256:], 64)
             w2_q.append(quantise(w2_g[g], f"w2_{g}"))
-            c_ = sb([P, S], U32, f"gw{g}")
-            nc.vector.tensor_copy(c_[:], xw[g][:].bitcast(U32).indirect(offs_t[:]))
-            gw.append(c_)
+        gw.append(pick_words(1))
 
-        def product(wq, tag):
+        def product(wq, tag, last_pieces):
             banks = [psum.tile([P, S], F32, name=f"{tag}{t}", tag=f"{tag}{t}") for t in range(PACK)]
-            for g in range(PASSES):
+            steps = [(0, 0, S)] + [(1, S * h // last_pieces, S * (h + 1) // last_pieces) for h in range(last_pieces)]
+            for g, a, b in steps:
                 for t in range(PACK):
                     cols = slice(P * t, P * (t + 1))
-                    nc.tensor.matmul_mx(out=banks[t][:], lhsT=wq[g][0][:, cols].bitcast(FP8X4), lhsT_scale=wq[g][1][:, cols],
-                                        rhs=gw[g][:].bitcast(FP8X4), rhs_scale=gs[g][:],
-                                        start=(g == 0), stop=(g == PASSES - 1))
+                    nc.tensor.matmul_mx(out=banks[t][:, a:b], lhsT=wq[g][0][:, cols].bitcast(FP8X4), lhsT_scale=wq[g][1][:, cols],
+                                        rhs=gw[g][:, a:b].bitcast(FP8X4), rhs_scale=gs[g][:, a:b],
+                                        start=(g == 0), stop=(g == PASSES - 1 and b == S))
             return banks
 
-        ag = product(w2_q, "ag")
+        ag = product(w2_q, "ag", 2)
         u = sb([P, PACK, S], F32, "u")
         for t in range(PACK):
             nc.scalar.activation(u[:, t, :], ag[t][:], ACT.Sigmoid, scale=-1.0)
@@ -123,9 +132,9 @@ def tile_picked_ysnowa_alb_p_kernel(tc, x_words, x_scales, w1, w2, dust, unit, w
         w1_q = []
         for g in range(PASSES):
             for h in range(2):
-                deal(nc.vector.tensor_copy, w1_g[g], w1_raw[g][h], 64 * h)
+                deal(nc.vector.tensor_copy, w1_g[g], w1_raw[g][h][:], 64 * h)
             w1_q.append(quantise(w1_g[g], f"w1_{g}"))
-        ts = product(w1_q, "ts")
+        ts = product(w1_q, "ts", 1)
         w3_g = sb([P, PACK * N], BF16, "w3_g")
         interleave(nc.vector.tensor_copy, w3_g, w3_raw)
         w3_q = quantise(w3_g, "w3")
@@ -174,10 +183,8 @@ def tile_picked_ysnowa_alb_p_kernel(tc, x_words, x_scales, w1, w2, dust, unit, w
             nc.vector.scalar_tensor_tensor(pb[:, t:t + 2, :], pa[:, t:t + 2, :], 1.0, u[:, t:t + 2, :], ALU.add, ALU.mult)
         num = sb([P, PACK, S], F32, "num")
 
-        def make_num(n):
-            c0, cw = CHUNKS[n]
-            cols = slice(c0, c0 + cw)
-            nc.vector.scalar_tensor_tensor(num[:, :, cols], pb[:, :, cols], 0.2, sgn[:, :, cols], ALU.add, ALU.mult)
+        for t in range(0, PACK, 2):
+            nc.vector.scalar_tensor_tensor(num[:, t:t + 2, :], pb[:, t:t + 2, :], 0.2, sgn[:, t:t + 2, :], ALU.add, ALU.mult)
 
         def make_hid(n):
             c0, cw = CHUNKS[n]
@@ -207,10 +214,7 @@ def tile_picked_ysnowa_alb_p_kernel(tc, x_words, x_scales, w1, w2, dust, unit, w
                     nc.scalar.copy(res[:], acc[:])
                 nc.sync.dma_start(out[cols, c0:c0 + cw], res[:])
 
-        make_num(0)
-        make_num(1)
         g0 = group(0, make_hid(0))
-        make_num(2)
         g1 = group(1, make_hid(1))
         z2 = make_hid(2)
         finish(0, g0)

@@ -36,17 +36,21 @@ def tile_picked_ysnowa_alb_p_kernel(tc, x_words, x_scales, w1, w2, dust, unit, w
         src_t = keep.tile([P, S // 16], U16, name="src_t")
         nc.sync.dma_start(offs_t[:], offs)
 
-        xs = sb([P, PASSES * T], U8, "xs")
-        nc.gpsimd.memset(xs[:, :T].bitcast(I32), 0)
-        nc.vector.memset(xs[:, T:].bitcast(I32), 0)
+        def staged(shape, dtype, name):
+            return keep.tile(shape, dtype, name=name, tag="stage", align_bytes=64)
+
+        xs = staged([P, T], U8, "xs")
+        nc.gpsimd.memset(xs[:].bitcast(I32), 0)
+        scale_rows = x_scales.bitcast(I32).rearrange("g (q r) c -> q g r c", r=4)
+        for q in range(4):
+            nc.gpsimd.dma_start(xs[32 * q:32 * q + 8, :].bitcast(I32), scale_rows[q])
         consts = sb([P, 2], F32, "consts")
         nc.vector.memset(consts[:, 0:1], 1.0)
         nc.vector.memset(consts[:, 1:2], TINY)
         one, tiny = consts[:, 0:1], consts[:, 1:2]
-        scale_rows = x_scales.bitcast(I32).rearrange("g (q r) c -> r q g c", r=4)
 
         def load_w(w, g, c0, c1, name):
-            raw = sb([P, PACK, c1 - c0], F32, name)
+            raw = keep.tile([P, PACK, c1 - c0], F32, name=name, tag=name, align_bytes=64)
             nc.sync.dma_start(raw[:], w[512 * g:512 * (g + 1), c0:c1].rearrange("(p j) c -> p j c", j=PACK))
             return raw
 
@@ -56,8 +60,6 @@ def tile_picked_ysnowa_alb_p_kernel(tc, x_words, x_scales, w1, w2, dust, unit, w
             return words
 
         xw = [load_x(0)]
-        for r in range(4):
-            nc.sync.dma_start(xs[r:P:32, :].bitcast(I32).rearrange("q (g c) -> q g c", g=PASSES), scale_rows[r])
         w2_raw = [load_w(w2, g, 0, H, f"w2_raw{g}") for g in range(PASSES)]
         xw.append(load_x(1))
         w1_raw = [[load_w(w1, g, 256 * h, 256 * (h + 1), f"w1_raw{g}{h}") for h in range(2)] for g in range(PASSES)]
@@ -89,11 +91,8 @@ def tile_picked_ysnowa_alb_p_kernel(tc, x_words, x_scales, w1, w2, dust, unit, w
             copy(grouped[:].rearrange("p (c i t) -> p c t i", t=PACK, i=4),
                  planes[:].rearrange("p t (c i) -> p c t i", i=4))
 
-        w2_g = [sb([P, PACK * H], BF16, f"w2_g{g}") for g in range(PASSES)]
-        for g in range(PASSES):
-            deal(nc.scalar.copy, w2_g[g], w2_raw[g][:, :, :256], 0)
         def pick_words(g):
-            picked = sb([P, S], U32, f"gw{g}")
+            picked = keep.tile([P, S], U32, name=f"gw{g}", tag="w2_raw1" if g else "gw0", align_bytes=64)
             pieces = 1 + g
             for h in range(pieces):
                 a, b = S * h // pieces, S * (h + 1) // pieces
@@ -101,15 +100,14 @@ def tile_picked_ysnowa_alb_p_kernel(tc, x_words, x_scales, w1, w2, dust, unit, w
             return picked
 
         gw = [pick_words(0)]
-        gs = []
-        for g in range(PASSES):
-            s_ = sb([P, S], U8, f"gs{g}")
-            nc.vector.tensor_copy(s_[:], xs[:, g * T:(g + 1) * T].indirect(offs_t[:]))
-            gs.append(s_)
+        gs = sb([P, S], U8, "gs")
+        nc.vector.tensor_copy(gs[:], xs[:].indirect(offs_t[:]))
         w2_q = []
         for g in range(PASSES):
-            deal(nc.vector.tensor_copy, w2_g[g], w2_raw[g][:, :, 256:], 64)
-            w2_q.append(quantise(w2_g[g], f"w2_{g}"))
+            grouped = staged([P, PACK * H], BF16, f"w2_g{g}")
+            deal(nc.scalar.copy, grouped, w2_raw[g][:, :, :256], 0)
+            deal(nc.vector.tensor_copy, grouped, w2_raw[g][:, :, 256:], 64)
+            w2_q.append(quantise(grouped, f"w2_{g}"))
         gw.append(pick_words(1))
 
         def product(wq, tag, last_pieces):
@@ -119,7 +117,7 @@ def tile_picked_ysnowa_alb_p_kernel(tc, x_words, x_scales, w1, w2, dust, unit, w
                 for t in range(PACK):
                     cols = slice(P * t, P * (t + 1))
                     nc.tensor.matmul_mx(out=banks[t][:, a:b], lhsT=wq[g][0][:, cols].bitcast(FP8X4), lhsT_scale=wq[g][1][:, cols],
-                                        rhs=gw[g][:, a:b].bitcast(FP8X4), rhs_scale=gs[g][:, a:b],
+                                        rhs=gw[g][:, a:b].bitcast(FP8X4), rhs_scale=gs[4 * g:, a:b],
                                         start=(g == 0), stop=(g == PASSES - 1 and b == S))
             return banks
 
@@ -128,14 +126,14 @@ def tile_picked_ysnowa_alb_p_kernel(tc, x_words, x_scales, w1, w2, dust, unit, w
         for t in range(PACK):
             nc.scalar.activation(u[:, t, :], ag[t][:], ACT.Sigmoid, scale=-1.0)
 
-        w1_g = [sb([P, PACK * H], BF16, f"w1_g{g}") for g in range(PASSES)]
         w1_q = []
         for g in range(PASSES):
+            grouped = staged([P, PACK * H], BF16, f"w1_g{g}")
             for h in range(2):
-                deal(nc.vector.tensor_copy, w1_g[g], w1_raw[g][h][:], 64 * h)
-            w1_q.append(quantise(w1_g[g], f"w1_{g}"))
+                deal(nc.vector.tensor_copy, grouped, w1_raw[g][h][:], 64 * h)
+            w1_q.append(quantise(grouped, f"w1_{g}"))
         ts = product(w1_q, "ts", 1)
-        w3_g = sb([P, PACK * N], BF16, "w3_g")
+        w3_g = staged([P, PACK * N], BF16, "w3_g")
         interleave(nc.vector.tensor_copy, w3_g, w3_raw)
         w3_q = quantise(w3_g, "w3")
 
@@ -151,7 +149,7 @@ def tile_picked_ysnowa_alb_p_kernel(tc, x_words, x_scales, w1, w2, dust, unit, w
 
         age = [sb([P, S + 16], F32, f"age{t}") for t in range(PACK)]
         for t in range(PACK):
-            nc.gpsimd.memset(age[t][:, S:], 0.0)
+            nc.vector.memset(age[t][:, S:], 0.0)
         dst = sb([P, PACK, S], F32, "dst")
 
         def make_age(t):
@@ -168,10 +166,8 @@ def tile_picked_ysnowa_alb_p_kernel(tc, x_words, x_scales, w1, w2, dust, unit, w
             nc.scalar.activation(den2[:, t, :], dst[:, t, :], ACT.Square, bias=one)
         rec = sb([P, PACK, S], F32, "rec")
         for c0, cw in CHUNKS:
-            nc.scalar.activation(rec[:, :, c0:c0 + cw], den2[:, :, c0:c0 + cw], ACT.Abs_reciprocal_sqrt)
+            nc.scalar.activation(rec[:, :, c0:c0 + cw], den2[:, :, c0:c0 + cw], ACT.Abs_reciprocal_sqrt, scale=0.25)
 
-        unit2 = sb([P, PACK], F32, "unit2")
-        nc.vector.tensor_scalar(unit2[:], unit_t[:], 2.0, None, ALU.mult)
         sgn = sb([P, PACK, S], F32, "sgn")
         for t in range(0, PACK, 2):
             nc.vector.tensor_scalar(sgn[:, t:t + 2, :], dst[:, t:t + 2, :], -1.0, 0.5, ALU.is_ge, ALU.subtract)
@@ -190,7 +186,7 @@ def tile_picked_ysnowa_alb_p_kernel(tc, x_words, x_scales, w1, w2, dust, unit, w
             c0, cw = CHUNKS[n]
             z = sb([P, PACK, cw], F32, f"hid{n}")
             for t in range(PACK):
-                nc.vector.scalar_tensor_tensor(z[:, t, :], num[:, t, c0:c0 + cw], unit2[:, t:t + 1], rec[:, t, c0:c0 + cw],
+                nc.vector.scalar_tensor_tensor(z[:, t, :], num[:, t, c0:c0 + cw], unit_t[:, t:t + 1], rec[:, t, c0:c0 + cw],
                                                ALU.mult, ALU.mult)
             return z
 

@@ -19,7 +19,8 @@ P = 128
 PACK = 4
 PASSES = K // (P * PACK)
 HALF = S // 2
-CHUNKS = ((0, 256), (256, 128), (384, 128))
+CHUNKS = ((0, 128), (128, 128), (256, 128), (384, 128))
+ON_SCALAR = 3
 TINY = 2.0 ** -60
 
 
@@ -39,11 +40,10 @@ def tile_picked_ysnowa_alb_p_kernel(tc, x_words, x_scales, w1, w2, dust, unit, w
         def staged(shape, dtype, name):
             return keep.tile(shape, dtype, name=name, tag="stage", align_bytes=64)
 
-        xs = staged([P, T], U8, "xs")
-        nc.gpsimd.memset(xs[:].bitcast(I32), 0)
+        xs = sb([P, T], U8, "xs")
+        nc.gpsimd.memset(xs[:, :T // 2].bitcast(I32), 0)
+        nc.vector.memset(xs[:, T // 2:].bitcast(I32), 0)
         scale_rows = x_scales.bitcast(I32).rearrange("g (q r) c -> q g r c", r=4)
-        for q in range(4):
-            nc.gpsimd.dma_start(xs[32 * q:32 * q + 8, :].bitcast(I32), scale_rows[q])
         consts = sb([P, 2], F32, "consts")
         nc.vector.memset(consts[:, 0:1], 1.0)
         nc.vector.memset(consts[:, 1:2], TINY)
@@ -60,18 +60,18 @@ def tile_picked_ysnowa_alb_p_kernel(tc, x_words, x_scales, w1, w2, dust, unit, w
             return words
 
         xw = [load_x(0)]
+        for q in range(4):
+            nc.sync.dma_start(xs[32 * q:32 * q + 8, :].bitcast(I32), scale_rows[q])
         w2_raw = [load_w(w2, g, 0, H, f"w2_raw{g}") for g in range(PASSES)]
         xw.append(load_x(1))
-        w1_raw = [[load_w(w1, g, 256 * h, 256 * (h + 1), f"w1_raw{g}{h}") for h in range(2)] for g in range(PASSES)]
+        w1_raw = [load_w(w1, g, 0, H, f"w1_raw{g}") for g in range(PASSES)]
+        nc.sync.dma_start(src_t[:], src)
+        dust_rows = dust.rearrange("(p t) j -> p t j", t=PACK)
+        dust_t = [sb([P, 2, S], F32, f"dust{h}") for h in range(2)]
+        nc.sync.dma_start(dust_t[0][:], dust_rows[:, 0:2, :])
         w3_raw = sb([P, PACK, N], F32, "w3_raw")
         nc.sync.dma_start(w3_raw[:], w3.rearrange("(p j) c -> p j c", j=PACK))
-        nc.sync.dma_start(src_t[:], src)
-        dust_rows = dust.rearrange("(p t) j -> t p j", t=PACK)
-        dust_t = []
-        for t in range(PACK):
-            d_ = sb([P, S], F32, f"dust{t}")
-            nc.sync.dma_start(d_[:], dust_rows[t])
-            dust_t.append(d_)
+        nc.sync.dma_start(dust_t[1][:], dust_rows[:, 2:4, :])
         unit_t = sb([P, PACK], F32, "unit_t")
         nc.sync.dma_start(unit_t[:], unit.rearrange("(p t) o -> p (t o)", t=PACK))
 
@@ -88,11 +88,11 @@ def tile_picked_ysnowa_alb_p_kernel(tc, x_words, x_scales, w1, w2, dust, unit, w
             return codes, scales
 
         def interleave(copy, grouped, planes):
-            copy(grouped[:].rearrange("p (c i t) -> p c t i", t=PACK, i=4),
-                 planes[:].rearrange("p t (c i) -> p c t i", i=4))
+            copy(grouped.rearrange("p (c i t) -> p c t i", t=PACK, i=4),
+                 planes.rearrange("p t (c i) -> p c t i", i=4))
 
         def pick_words(g):
-            picked = keep.tile([P, S], U32, name=f"gw{g}", tag="w2_raw1" if g else "gw0", align_bytes=64)
+            picked = keep.tile([P, S], U32, name=f"gw{g}", align_bytes=64)
             pieces = 1 + g
             for h in range(pieces):
                 a, b = S * h // pieces, S * (h + 1) // pieces
@@ -112,13 +112,14 @@ def tile_picked_ysnowa_alb_p_kernel(tc, x_words, x_scales, w1, w2, dust, unit, w
 
         def product(wq, tag, last_pieces):
             banks = [psum.tile([P, S], F32, name=f"{tag}{t}", tag=f"{tag}{t}") for t in range(PACK)]
-            steps = [(0, 0, S)] + [(1, S * h // last_pieces, S * (h + 1) // last_pieces) for h in range(last_pieces)]
-            for g, a, b in steps:
-                for t in range(PACK):
-                    cols = slice(P * t, P * (t + 1))
-                    nc.tensor.matmul_mx(out=banks[t][:, a:b], lhsT=wq[g][0][:, cols].bitcast(FP8X4), lhsT_scale=wq[g][1][:, cols],
-                                        rhs=gw[g][:, a:b].bitcast(FP8X4), rhs_scale=gs[4 * g:, a:b],
-                                        start=(g == 0), stop=(g == PASSES - 1 and b == S))
+            steps = [(0, t, 0, S) for t in range(PACK)]
+            for pair in ((0, 1), (2, 3)):
+                steps.extend((1, t, S * h // last_pieces, S * (h + 1) // last_pieces) for h in range(last_pieces) for t in pair)
+            for g, t, a, b in steps:
+                cols = slice(P * t, P * (t + 1))
+                nc.tensor.matmul_mx(out=banks[t][:, a:b], lhsT=wq[g][0][:, cols].bitcast(FP8X4), lhsT_scale=wq[g][1][:, cols],
+                                    rhs=gw[g][:, a:b].bitcast(FP8X4), rhs_scale=gs[4 * g:, a:b],
+                                    start=(g == 0), stop=(g == PASSES - 1 and b == S))
             return banks
 
         ag = product(w2_q, "ag", 2)
@@ -129,13 +130,9 @@ def tile_picked_ysnowa_alb_p_kernel(tc, x_words, x_scales, w1, w2, dust, unit, w
         w1_q = []
         for g in range(PASSES):
             grouped = staged([P, PACK * H], BF16, f"w1_g{g}")
-            for h in range(2):
-                deal(nc.vector.tensor_copy, grouped, w1_raw[g][h][:], 64 * h)
+            deal(nc.vector.tensor_copy, grouped, w1_raw[g][:], 0)
             w1_q.append(quantise(grouped, f"w1_{g}"))
         ts = product(w1_q, "ts", 1)
-        w3_g = staged([P, PACK * N], BF16, "w3_g")
-        interleave(nc.vector.tensor_copy, w3_g, w3_raw)
-        w3_q = quantise(w3_g, "w3")
 
         lnu = sb([P, PACK, S], F32, "lnu")
         for t in range(PACK):
@@ -149,7 +146,7 @@ def tile_picked_ysnowa_alb_p_kernel(tc, x_words, x_scales, w1, w2, dust, unit, w
 
         age = [sb([P, S + 16], F32, f"age{t}") for t in range(PACK)]
         for t in range(PACK):
-            nc.vector.memset(age[t][:, S:], 0.0)
+            nc.gpsimd.memset(age[t][:, S:], 0.0)
         dst = sb([P, PACK, S], F32, "dst")
 
         def make_age(t):
@@ -159,11 +156,13 @@ def tile_picked_ysnowa_alb_p_kernel(tc, x_words, x_scales, w1, w2, dust, unit, w
         for t in range(PACK):
             if t + 1 < PACK:
                 make_age(t + 1)
-            nc.vector.tensor_tensor(dst[:, t, :], age[t][:].indirect(src_t[:]), dust_t[t][:], ALU.mult)
+            nc.vector.tensor_tensor(dst[:, t, :], age[t][:].indirect(src_t[:]), dust_t[t // 2][:, t % 2, :], ALU.mult)
 
         den2 = sb([P, PACK, S], F32, "den2")
         for t in range(PACK):
             nc.scalar.activation(den2[:, t, :], dst[:, t, :], ACT.Square, bias=one)
+        w3_g = sb([P, PACK * N], BF16, "w3_g")
+        interleave(nc.scalar.copy, w3_g[:, :PACK * P], w3_raw[:, :, :P])
         rec = sb([P, PACK, S], F32, "rec")
         for c0, cw in CHUNKS:
             nc.scalar.activation(rec[:, :, c0:c0 + cw], den2[:, :, c0:c0 + cw], ACT.Abs_reciprocal_sqrt, scale=0.25)
@@ -182,6 +181,9 @@ def tile_picked_ysnowa_alb_p_kernel(tc, x_words, x_scales, w1, w2, dust, unit, w
         for t in range(0, PACK, 2):
             nc.vector.scalar_tensor_tensor(num[:, t:t + 2, :], pb[:, t:t + 2, :], 0.2, sgn[:, t:t + 2, :], ALU.add, ALU.mult)
 
+        interleave(nc.vector.tensor_copy, w3_g[:, PACK * P:], w3_raw[:, :, P:])
+        w3_q = quantise(w3_g, "w3")
+
         def make_hid(n):
             c0, cw = CHUNKS[n]
             z = sb([P, PACK, cw], F32, f"hid{n}")
@@ -192,28 +194,25 @@ def tile_picked_ysnowa_alb_p_kernel(tc, x_words, x_scales, w1, w2, dust, unit, w
 
         def group(n, z):
             zg = sb([P, PACK * CHUNKS[n][1]], BF16, f"hid_g{n}")
-            interleave(nc.vector.tensor_copy if n == len(CHUNKS) - 1 else nc.scalar.copy, zg, z)
+            interleave(nc.vector.tensor_copy if n >= ON_SCALAR else nc.scalar.copy, zg[:], z[:])
             return zg
 
         def finish(n, zg):
             c0, cw = CHUNKS[n]
             codes, scales = quantise(zg, f"hid{n}")
+            acc = psum.tile([P, N // P, cw], F32, name=f"acc{n}", tag=f"ag{n}")
             for b in range(N // P):
-                acc = psum.tile([P, cw], F32, name=f"acc{n}{b}", tag=f"ag{(2 * n + b) % PACK}")
                 cols = slice(P * b, P * (b + 1))
-                nc.tensor.matmul_mx(out=acc[:], lhsT=w3_q[0][:, cols].bitcast(FP8X4), lhsT_scale=w3_q[1][:, cols],
+                nc.tensor.matmul_mx(out=acc[:, b, :], lhsT=w3_q[0][:, cols].bitcast(FP8X4), lhsT_scale=w3_q[1][:, cols],
                                     rhs=codes[:].bitcast(FP8X4), rhs_scale=scales[:], start=True, stop=True)
-                res = sb([P, cw], F32, f"res{n}{b}")
-                if b == 1 and n == len(CHUNKS) - 1:
-                    nc.vector.tensor_copy(res[:], acc[:])
-                else:
-                    nc.scalar.copy(res[:], acc[:])
-                nc.sync.dma_start(out[cols, c0:c0 + cw], res[:])
+            res = sb([P, N // P, cw], F32, f"res{n}")
+            evacuate = nc.vector.tensor_copy if n == len(CHUNKS) - 2 else nc.scalar.copy
+            evacuate(res[:], acc[:])
+            nc.sync.dma_start(out[:, c0:c0 + cw].rearrange("(b p) c -> p b c", p=P), res[:])
 
-        g0 = group(0, make_hid(0))
-        g1 = group(1, make_hid(1))
-        z2 = make_hid(2)
-        finish(0, g0)
-        g2 = group(2, z2)
-        finish(1, g1)
-        finish(2, g2)
+        planes = [make_hid(n) for n in range(len(CHUNKS))]
+        grouped = [group(n, planes[n]) for n in range(ON_SCALAR)]
+        finish(0, grouped[0])
+        grouped.append(group(3, planes[3]))
+        for n in range(1, len(CHUNKS)):
+            finish(n, grouped[n])

from contextlib import ExitStack

import concourse.mybir as mybir

K, T, S, N, H = 1024, 2048, 512, 256, 512
FLOPS = 2 * (2 * K * H * S + H * N * S)

F32 = mybir.dt.float32
BF16 = mybir.dt.bfloat16
I32 = mybir.dt.int32
U32 = mybir.dt.uint32
U16 = mybir.dt.uint16
U8 = mybir.dt.uint8
FP8X4 = mybir.dt.float8_e4m3fn_x4
ACT = mybir.ActivationFunctionType
ALU = mybir.AluOpType

P = 128
PACK = 4
PASSES = K // (P * PACK)
HALF = S // 2
CHUNKS = ((0, 128), (128, 128), (256, 128), (384, 128))
ON_SCALAR = 3
TINY = 2.0 ** -60


def tile_picked_ysnowa_alb_p_kernel(tc, x_words, x_scales, w1, w2, dust, unit, w3, offs, src, out):
    nc = tc.nc
    with ExitStack() as ctx:
        keep = ctx.enter_context(tc.tile_pool(name="keep", bufs=1))
        psum = ctx.enter_context(tc.psum_pool(name="psum", bufs=1))

        def sb(shape, dtype, name):
            return keep.tile(shape, dtype, name=name, align_bytes=64)

        offs_t = keep.tile([P, S // 16], U16, name="offs_t")
        src_t = keep.tile([P, S // 16], U16, name="src_t")
        nc.sync.dma_start(offs_t[:], offs)

        def staged(shape, dtype, name):
            return keep.tile(shape, dtype, name=name, tag="stage", align_bytes=64)

        xs = sb([P, T], U8, "xs")
        nc.gpsimd.memset(xs[:, :T // 2].bitcast(I32), 0)
        nc.vector.memset(xs[:, T // 2:].bitcast(I32), 0)
        scale_rows = x_scales.bitcast(I32).rearrange("g (q r) c -> q g r c", r=4)
        consts = sb([P, 2], F32, "consts")
        nc.vector.memset(consts[:, 0:1], 1.0)
        nc.vector.memset(consts[:, 1:2], TINY)
        one, tiny = consts[:, 0:1], consts[:, 1:2]

        def load_w(w, g, c0, c1, name):
            raw = keep.tile([P, PACK, c1 - c0], F32, name=name, tag=name, align_bytes=64)
            nc.sync.dma_start(raw[:], w[512 * g:512 * (g + 1), c0:c1].rearrange("(p j) c -> p j c", j=PACK))
            return raw

        def load_x(g):
            words = sb([P, T], I32, f"xw{g}")
            nc.sync.dma_start(words[:], x_words[g].rearrange("p n t -> p (n t)").bitcast(I32))
            return words

        xw = [load_x(0)]
        for q in range(4):
            nc.sync.dma_start(xs[32 * q:32 * q + 8, :].bitcast(I32), scale_rows[q])
        w2_raw = [load_w(w2, g, 0, H, f"w2_raw{g}") for g in range(PASSES)]
        xw.append(load_x(1))
        w1_raw = [load_w(w1, g, 0, H, f"w1_raw{g}") for g in range(PASSES)]
        nc.sync.dma_start(src_t[:], src)
        dust_rows = dust.rearrange("(p t) j -> p t j", t=PACK)
        dust_t = [sb([P, 2, S], F32, f"dust{h}") for h in range(2)]
        nc.sync.dma_start(dust_t[0][:], dust_rows[:, 0:2, :])
        w3_raw = sb([P, PACK, N], F32, "w3_raw")
        nc.sync.dma_start(w3_raw[:], w3.rearrange("(p j) c -> p j c", j=PACK))
        nc.sync.dma_start(dust_t[1][:], dust_rows[:, 2:4, :])
        unit_t = sb([P, PACK], F32, "unit_t")
        nc.sync.dma_start(unit_t[:], unit.rearrange("(p t) o -> p (t o)", t=PACK))

        def deal(copy, grouped, raw, m0):
            width = raw.shape[2] // PACK
            copy(grouped[:].rearrange("p (t m j) -> p m j t", t=PACK, j=PACK)[:, m0:m0 + width],
                 raw.rearrange("p j (m t) -> p m j t", t=PACK))

        def quantise(grouped, name):
            width = grouped.shape[1] // PACK
            codes = sb([P, width], U32, name + "_codes")
            scales = sb([P, width], U8, name + "_scales")
            nc.vector.quantize_mx(out=codes[:].bitcast(FP8X4), scales=scales[:], in_=grouped[:])
            return codes, scales

        def interleave(copy, grouped, planes):
            copy(grouped.rearrange("p (c i t) -> p c t i", t=PACK, i=4),
                 planes.rearrange("p t (c i) -> p c t i", i=4))

        def pick_words(g):
            picked = keep.tile([P, S], U32, name=f"gw{g}", align_bytes=64)
            pieces = 1 + g
            for h in range(pieces):
                a, b = S * h // pieces, S * (h + 1) // pieces
                nc.vector.tensor_copy(picked[:, a:b], xw[g][:].bitcast(U32).indirect(offs_t[:, a // 16:b // 16]))
            return picked

        gw = [pick_words(0)]
        gs = sb([P, S], U8, "gs")
        nc.vector.tensor_copy(gs[:], xs[:].indirect(offs_t[:]))
        w2_q = []
        for g in range(PASSES):
            grouped = staged([P, PACK * H], BF16, f"w2_g{g}")
            deal(nc.scalar.copy, grouped, w2_raw[g][:, :, :256], 0)
            deal(nc.vector.tensor_copy, grouped, w2_raw[g][:, :, 256:], 64)
            w2_q.append(quantise(grouped, f"w2_{g}"))
        gw.append(pick_words(1))

        def product(wq, tag, last_pieces):
            banks = [psum.tile([P, S], F32, name=f"{tag}{t}", tag=f"{tag}{t}") for t in range(PACK)]
            steps = [(0, t, 0, S) for t in range(PACK)]
            for pair in ((0, 1), (2, 3)):
                steps.extend((1, t, S * h // last_pieces, S * (h + 1) // last_pieces) for h in range(last_pieces) for t in pair)
            for g, t, a, b in steps:
                cols = slice(P * t, P * (t + 1))
                nc.tensor.matmul_mx(out=banks[t][:, a:b], lhsT=wq[g][0][:, cols].bitcast(FP8X4), lhsT_scale=wq[g][1][:, cols],
                                    rhs=gw[g][:, a:b].bitcast(FP8X4), rhs_scale=gs[4 * g:, a:b],
                                    start=(g == 0), stop=(g == PASSES - 1 and b == S))
            return banks

        ag = product(w2_q, "ag", 2)
        u = sb([P, PACK, S], F32, "u")
        for t in range(PACK):
            nc.scalar.activation(u[:, t, :], ag[t][:], ACT.Sigmoid, scale=-1.0)

        w1_q = []
        for g in range(PASSES):
            grouped = staged([P, PACK * H], BF16, f"w1_g{g}")
            deal(nc.vector.tensor_copy, grouped, w1_raw[g][:], 0)
            w1_q.append(quantise(grouped, f"w1_{g}"))
        ts = product(w1_q, "ts", 1)

        lnu = sb([P, PACK, S], F32, "lnu")
        for t in range(PACK):
            nc.scalar.activation(lnu[:, t, :], u[:, t, :], ACT.Ln, bias=tiny)
        wr = sb([P, PACK, S], F32, "wr")
        for t in range(0, PACK, 2):
            nc.scalar.activation(wr[:, t:t + 2, :], lnu[:, t:t + 2, :], ACT.Exp, scale=0.8)
        melt = sb([P, PACK, S], F32, "melt")
        for t in range(PACK):
            nc.scalar.activation(melt[:, t, :], ts[t][:], ACT.Sigmoid, scale=2.0)

        age = [sb([P, S + 16], F32, f"age{t}") for t in range(PACK)]
        for t in range(PACK):
            nc.gpsimd.memset(age[t][:, S:], 0.0)
        dst = sb([P, PACK, S], F32, "dst")

        def make_age(t):
            nc.vector.scalar_tensor_tensor(age[t][:, :S], lnu[:, t, :], -1.0, ag[t][:], ALU.mult, ALU.max)

        make_age(0)
        for t in range(PACK):
            if t + 1 < PACK:
                make_age(t + 1)
            nc.vector.tensor_tensor(dst[:, t, :], age[t][:].indirect(src_t[:]), dust_t[t // 2][:, t % 2, :], ALU.mult)

        den2 = sb([P, PACK, S], F32, "den2")
        for t in range(PACK):
            nc.scalar.activation(den2[:, t, :], dst[:, t, :], ACT.Square, bias=one)
        w3_g = sb([P, PACK * N], BF16, "w3_g")
        interleave(nc.scalar.copy, w3_g[:, :PACK * P], w3_raw[:, :, :P])
        rec = sb([P, PACK, S], F32, "rec")
        for c0, cw in CHUNKS:
            nc.scalar.activation(rec[:, :, c0:c0 + cw], den2[:, :, c0:c0 + cw], ACT.Abs_reciprocal_sqrt, scale=0.25)

        sgn = sb([P, PACK, S], F32, "sgn")
        for t in range(0, PACK, 2):
            nc.vector.tensor_scalar(sgn[:, t:t + 2, :], dst[:, t:t + 2, :], -1.0, 0.5, ALU.is_ge, ALU.subtract)
        pa = sb([P, PACK, S], F32, "pa")
        pb = sb([P, PACK, S], F32, "pb")
        for t in range(0, PACK, 2):
            nc.vector.scalar_tensor_tensor(pa[:, t:t + 2, :], wr[:, t:t + 2, :], -1.0, melt[:, t:t + 2, :], ALU.add, ALU.mult)
        for t in range(0, PACK, 2):
            nc.vector.scalar_tensor_tensor(pb[:, t:t + 2, :], pa[:, t:t + 2, :], 1.0, u[:, t:t + 2, :], ALU.add, ALU.mult)
        num = sb([P, PACK, S], F32, "num")

        for t in range(0, PACK, 2):
            nc.vector.scalar_tensor_tensor(num[:, t:t + 2, :], pb[:, t:t + 2, :], 0.2, sgn[:, t:t + 2, :], ALU.add, ALU.mult)

        interleave(nc.vector.tensor_copy, w3_g[:, PACK * P:], w3_raw[:, :, P:])
        w3_q = quantise(w3_g, "w3")

        def make_hid(n):
            c0, cw = CHUNKS[n]
            z = sb([P, PACK, cw], F32, f"hid{n}")
            for t in range(PACK):
                nc.vector.scalar_tensor_tensor(z[:, t, :], num[:, t, c0:c0 + cw], unit_t[:, t:t + 1], rec[:, t, c0:c0 + cw],
                                               ALU.mult, ALU.mult)
            return z

        def group(n, z):
            zg = sb([P, PACK * CHUNKS[n][1]], BF16, f"hid_g{n}")
            interleave(nc.vector.tensor_copy if n >= ON_SCALAR else nc.scalar.copy, zg[:], z[:])
            return zg

        def finish(n, zg):
            c0, cw = CHUNKS[n]
            codes, scales = quantise(zg, f"hid{n}")
            acc = psum.tile([P, N // P, cw], F32, name=f"acc{n}", tag=f"ag{n}")
            for b in range(N // P):
                cols = slice(P * b, P * (b + 1))
                nc.tensor.matmul_mx(out=acc[:, b, :], lhsT=w3_q[0][:, cols].bitcast(FP8X4), lhsT_scale=w3_q[1][:, cols],
                                    rhs=codes[:].bitcast(FP8X4), rhs_scale=scales[:], start=True, stop=True)
            res = sb([P, N // P, cw], F32, f"res{n}")
            evacuate = nc.vector.tensor_copy if n == len(CHUNKS) - 2 else nc.scalar.copy
            evacuate(res[:], acc[:])
            nc.sync.dma_start(out[:, c0:c0 + cw].rearrange("(b p) c -> p b c", p=P), res[:])

        planes = [make_hid(n) for n in range(len(CHUNKS))]
        grouped = [group(n, planes[n]) for n in range(ON_SCALAR)]
        finish(0, grouped[0])
        grouped.append(group(3, planes[3]))
        for n in range(1, len(CHUNKS)):
            finish(n, grouped[n])
